import numpy as np
import ml_dtypes


def mxq(x, axis, fmt="e4m3"):
    dtype, down = {"e4m3": (ml_dtypes.float8_e4m3fn, 7), "e5m2": (ml_dtypes.float8_e5m2, 14)}[fmt]
    v = np.moveaxis(np.asarray(x, np.float32).astype(ml_dtypes.bfloat16).astype(np.float64), axis, -1)
    blocks = v.reshape(v.shape[:-1] + (-1, 32))
    amax = np.abs(blocks).max(-1, keepdims=True)
    byte = np.maximum(np.where(amax > 0, np.frexp(amax)[1] - 1 + 127, 0) - down, 1)
    scale = np.exp2(byte - 127.0)
    codes = (blocks / scale).astype(np.float32).astype(dtype).astype(np.float64)
    return np.moveaxis((codes * scale).reshape(v.shape), -1, axis)


WIDE = False


def mx_kscale(k):
    if not WIDE:
        return np.ones(k)
    levels = np.array([10, -10, 5, -5, 0])
    if k % 512:
        return np.exp2(np.random.permutation(np.resize(levels, k // 32))).repeat(32)
    a = np.empty((k // 512, 16))
    for p in range(k // 512):
        a[p, :8] = np.random.permutation(np.resize(levels, 8))
        for g in range(8):
            far = levels[np.abs(levels - a[p, g]) >= 10]
            a[p, g + 8] = far[np.random.randint(len(far))]
    return np.exp2(a.ravel()).repeat(32)


def f64(x):
    return np.asarray(x).astype(np.float64)


def striped(idx):
    return np.tile(idx.reshape(-1, 16).T, (8, 1)).astype(np.uint16)


def unstriped(offs):
    return offs[:16].T.reshape(-1).astype(np.int64)


def striped8(idx):
    return np.concatenate([x.reshape(-1, 16).T for x in idx]).astype(np.uint16)


def runs(offs, k):
    lists = np.stack([offs[16 * r : 16 * r + 16].T.reshape(-1) for r in range(8)]).astype(np.int64)
    return lists[np.arange(k) % 512 // 64]


def pack_weight(w):
    k, n = w.shape
    w = f64(np.asarray(w, np.float32).astype(ml_dtypes.bfloat16)).reshape(k // 32, 32, n)
    amax = np.abs(w).max(1)
    byte = np.clip(np.where(amax > 0, np.frexp(amax)[1] - 1 + 127 - 7, 1), 1, 254)
    scaled = (w * np.exp2(127.0 - byte)[:, None, :]).reshape(k, n).astype(np.float32)
    words = np.ascontiguousarray(scaled.reshape(k // 512, 128, 4, n).transpose(0, 1, 3, 2)).astype(ml_dtypes.float8_e4m3fn).view(np.uint8)
    return words, np.ascontiguousarray(byte.astype(np.uint8).reshape(k // 512, 16, n))


def unpack_weight(words, scales):
    g, p, n, _ = words.shape
    vals = np.ascontiguousarray(words).view(ml_dtypes.float8_e4m3fn).astype(np.float64) * np.repeat(np.exp2(scales.astype(np.float64) - 127.0), 8, axis=1)[..., None]
    return vals.transpose(0, 1, 3, 2).reshape(g * 512, n)


def sigmoid(v):
    return 1.0 / (1.0 + np.exp(-np.maximum(v, -700.0)))


K, T, S, N, G, H, W = 512, 1024, 256, 512, 2048, 512, 128


def setup_inputs():
    n = np.random.standard_normal
    s = mx_kscale(K)[:, None]
    u = mx_kscale(K)
    packed_xT = pack_weight(n((K, T)) * s)
    packed_dT = pack_weight(n((K, G)) / s)
    perm = np.random.permutation(S)
    perm2 = np.random.permutation(S)
    return {
        "x_words": packed_xT[0],
        "x_scales": packed_xT[1],
        "d_words": packed_dT[0],
        "d_scales": packed_dT[1],
        "sl": np.random.uniform(1.0, 2.0, (H, 1)).astype(np.float32),
        "th": (0.5 * n((H, 1))).astype(np.float32),
        "gn": (np.random.uniform(0.5, 1.5, (H, 1)) * u[:, None]).astype(np.float32),
        "w1": (n((H, N)) / np.sqrt(2 * H) / u[:, None]).astype(np.float32),
        "w2": (n((K, N)) / np.sqrt(2 * K) / s).astype(np.float32),
        "offs": striped(np.random.permutation(T)[:S]),
        "k1": striped8(np.random.randint(0, G, (8, H))),
        "hz": striped8(np.random.randint(0, T, (8, S))),
        "k2": striped8(np.random.randint(0, G, (8, H))),
        "hy": striped8(np.random.randint(0, T, (8, S))),
        "k3": striped8(np.random.randint(0, G, (8, H))),
        "n1": striped(np.random.permutation(S)),
        "n2": striped(np.random.permutation(S)),
        "two": striped(np.random.permutation(T)[:S]),
        "n3": striped(perm[:W]),
        "n4": striped(perm[W:]),
        "n5": striped(perm2[:W]),
        "n6": striped(perm2[W:]),
        "n7": striped(np.random.permutation(S)),
    }


def reference(x_words, x_scales, d_words, d_scales, sl, th, gn, w1, w2, offs, k1, hz, k2, hy, k3, n1, n2, two, n3, n4, n5, n6, n7):
    d_k1 = unpack_weight(d_words, d_scales)[np.arange(K)[:, None], runs(k1, K)]
    xq = unpack_weight(x_words, x_scales)[:, unstriped(offs)]
    d_k2 = unpack_weight(d_words, d_scales)[np.arange(K)[:, None], runs(k2, K)]
    x_hz = unpack_weight(x_words, x_scales)[np.arange(K)[:, None], runs(hz, K)]
    d_k3 = unpack_weight(d_words, d_scales)[np.arange(K)[:, None], runs(k3, K)]
    x_hy = unpack_weight(x_words, x_scales)[np.arange(K)[:, None], runs(hy, K)]
    h = 0.0625 * (d_k1.T @ xq + d_k2.T @ x_hz + d_k3.T @ x_hy)
    ds = np.zeros((H, S))
    ds[:, unstriped(n1)] = h
    sg = sigmoid(f64(sl) * (ds[:, unstriped(n2)] - f64(th)))
    z = f64(gn) * (h * sg)
    x_two = unpack_weight(x_words, x_scales)[:, unstriped(two)]
    h2 = mxq(f64(w1), 0, "e4m3").T @ mxq(z, 0, "e4m3") + mxq(f64(w2), 0, "e4m3").T @ x_two
    pa = h2[:, unstriped(n3)]
    pb = h2[:, unstriped(n4)]
    rb = np.maximum(pa, pb)
    ua = np.zeros((N, S))
    ua[:, unstriped(n5)] = pb
    ub = ua.copy()
    ub[:, unstriped(n6)] = rb
    return ub - h2[:, unstriped(n7)]

@@ -1,0 +1,275 @@
+from contextlib import ExitStack
+
+import concourse.mybir as mybir
+from concourse.masks import make_identity
+
+F32 = mybir.dt.float32
+BF16 = mybir.dt.bfloat16
+I32 = mybir.dt.int32
+U32 = mybir.dt.uint32
+U16 = mybir.dt.uint16
+U8 = mybir.dt.uint8
+FP8X4 = mybir.dt.float8_e4m3fn_x4
+ALU = mybir.AluOpType
+ACT = mybir.ActivationFunctionType
+
+P = 128
+K, T, S, N, G, H, W = 512, 1024, 256, 512, 2048, 512, 128
+HALF = 256
+FLOPS = 2 * (3 * K * H * S + H * N * S + K * N * S)
+
+
+def tile_picked_mthhznterlcpsw_none_p_kernel(
+    tc, x_words, x_scales, d_words, d_scales, sl, th, gn, w1, w2,
+    offs, k1, hz, k2, hy, k3, n1, n2, two, n3, n4, n5, n6, n7, out,
+):
+    nc = tc.nc
+    with ExitStack() as ctx:
+        lists = ctx.enter_context(tc.tile_pool(name="lists", bufs=1))
+        keep = ctx.enter_context(tc.tile_pool(name="keep", bufs=1))
+        psum = ctx.enter_context(tc.psum_pool(name="psum", bufs=1))
+
+        def load_list(name, src):
+            tile = lists.tile(list(src.shape), U16, name=name)
+            nc.sync.dma_start(out=tile[:], in_=src)
+            return tile
+
+        def load_scale_table(name, src, cols):
+            tile = keep.tile([P, cols], U8, name=name)
+            rows = src[0].bitcast(I32).unsqueeze(1).broadcast_to([16, 8, cols // 4])
+            nc.scalar.dma_start(out=tile[:].bitcast(I32), in_=rows)
+            return tile
+
+        def load_word_table(name, src, cols):
+            tile = keep.tile([P, cols], I32, name=name)
+            nc.sync.dma_start(out=tile[:], in_=src[0].rearrange("p c r -> p (c r)").bitcast(I32))
+            return tile
+
+        x_scale_table = load_scale_table("x_scale_table", x_scales, T)
+        d_scale_table = load_scale_table("d_scale_table", d_scales, G)
+        token_lists = [load_list("offs", offs)]
+        code_lists = [load_list("k1", k1), load_list("k2", k2), load_list("k3", k3)]
+        token_lists += [load_list("hz", hz), load_list("hy", hy)]
+        d_word_table = load_word_table("d_word_table", d_words, G)
+        x_word_table = load_word_table("x_word_table", x_words, T)
+
+        vector_rows = keep.tile([P, P], F32, name="vector_rows")
+        nc.gpsimd.memset(vector_rows[:], 0.0)
+        ident_f32 = keep.tile([P, P], F32, name="ident_f32")
+        make_identity(nc, ident_f32[:])
+        for v, src in enumerate((sl, th, gn)):
+            nc.gpsimd.dma_start(out=vector_rows[4 * v : 4 * v + 4, :], in_=src.rearrange("(a p) o -> a (p o)", p=P))
+        ident_bf = keep.tile([P, P], BF16, name="ident_bf")
+        make_identity(nc, ident_bf[:])
+        vector_bank = psum.tile([P, P], F32, name="vector_bank", tag="back_bank0")
+        nc.tensor.transpose(vector_bank[:], vector_rows[:], ident_f32[:])
+        per_row = keep.tile([P, 12], F32, name="per_row")
+        nc.scalar.activation(out=per_row[:], in_=vector_bank[:, :12], func=ACT.Copy)
+        slope, thresh, gain = per_row[:, 0:4], per_row[:, 4:8], per_row[:, 8:12]
+
+        first_planes = keep.tile([P, 6 * HALF], U8, name="first_planes", align_bytes=64)
+        second_planes = keep.tile([P, 3 * HALF], U8, name="second_planes", align_bytes=64)
+        two_plane = keep.tile([P, S], U8, name="two_plane", align_bytes=64)
+        for planes in (first_planes, second_planes, two_plane):
+            nc.vector.memset(planes[:].bitcast(I32), 0)
+
+        def gather_scales(name, tag, picks, planes):
+            picked = keep.tile([P, len(picks) * HALF], U8, name=name, tag=tag, align_bytes=64)
+            for c, table, offsets in picks:
+                nc.vector.tensor_copy(out=picked[:, c * HALF : (c + 1) * HALF], in_=table[:].indirect(offsets))
+            for j in range(4):
+                nc.sync.dma_start(out=planes[j:P:32, :].bitcast(I32), in_=picked[8 * j : P : 32, :].bitcast(I32))
+
+        def gather_words(name, tag, table, offsets):
+            picked = keep.tile([P, HALF], U32, name=name, tag=tag, align_bytes=64)
+            nc.vector.tensor_copy(out=picked[:], in_=table[:].bitcast(U32).indirect(offsets))
+            return picked
+
+        def code_half(c, half):
+            return code_lists[c][:, 16 * half : 16 * (half + 1)]
+
+        gather_scales(
+            "first_picked",
+            "picked_scales",
+            [(3, x_scale_table, token_lists[0][:])]
+            + [(c, d_scale_table, code_half(c, 0)) for c in range(3)]
+            + [(3 + c, x_scale_table, token_lists[c][:]) for c in (1, 2)],
+            first_planes,
+        )
+        n1_list = load_list("n1", n1)
+        n2_list = load_list("n2", n2)
+        two_list = load_list("two", two)
+        n4_list = load_list("n4", n4)
+        n3_list = load_list("n3", n3)
+        n5_list = load_list("n5", n5)
+        n7_list = load_list("n7", n7)
+        n6_list = load_list("n6", n6)
+        w_raw = []
+        for name, w in (("w1_raw", w1), ("w2_raw", w2)):
+            raw = keep.tile([P, 4, N], F32, name=name)
+            nc.sync.dma_start(out=raw[:], in_=w.rearrange("(p t) m -> p t m", t=4))
+            w_raw.append(raw)
+        code_words = [gather_words(f"code_words{c}_0", f"code_words{c}", d_word_table, code_half(c, 0)) for c in range(3)]
+        token_words = [keep.tile([P, S], U32, name=f"token_words{c}", tag=f"token_words{c}", align_bytes=64) for c in range(3)]
+        for jh in range(2):
+            for c in range(3):
+                nc.vector.tensor_copy(
+                    out=token_words[c][:, jh * P : (jh + 1) * P],
+                    in_=x_word_table[:].bitcast(U32).indirect(token_lists[c][:, 8 * jh : 8 * (jh + 1)]),
+                )
+        token_planes = [first_planes[:, (3 + c) * HALF : (4 + c) * HALF] for c in range(3)]
+
+        slope_thresh = keep.tile([P, 4], F32, name="slope_thresh")
+        bias = keep.tile([P, 4], F32, name="bias")
+        nc.gpsimd.tensor_tensor(out=slope_thresh[:], in0=slope, in1=thresh, op=ALU.mult)
+        nc.gpsimd.tensor_scalar(out=bias[:], in0=slope_thresh[:], scalar1=-1.0, scalar2=0.0, op0=ALU.mult, op1=ALU.add)
+
+        h_rows = [keep.tile([P, S], F32, name=f"h_rows{a}") for a in range(4)]
+        ds_rows = [keep.tile([P, 2 * S], F32, name=f"ds_rows{a}") for a in range(4)]
+        sg_rows = [keep.tile([P, S], F32, name=f"sg_rows{a}") for a in range(4)]
+        z_turned = [keep.tile([P, 2, P], F32, name=f"z_turned{jh}") for jh in range(2)]
+
+        def first_pass(bank, words, planes, c, r, cols):
+            nc.tensor.matmul_mx(
+                out=bank,
+                lhsT=words[c][:, r * P : (r + 1) * P].bitcast(FP8X4),
+                lhsT_scale=planes[:, c * HALF + r * P : c * HALF + (r + 1) * P],
+                rhs=token_words[c][:, cols].bitcast(FP8X4),
+                rhs_scale=token_planes[c][:, cols],
+                start=(c == 0),
+                stop=(c == 2),
+            )
+
+        def gate(a, jh):
+            cols = slice(jh * P, (jh + 1) * P)
+            nc.scalar.activation(
+                out=sg_rows[a][:, cols],
+                in_=ds_rows[a][:].indirect(n2_list[:, 8 * jh : 8 * (jh + 1)]),
+                func=ACT.Sigmoid,
+                scale=slope[:, a : a + 1],
+                bias=bias[:, a : a + 1],
+            )
+            nc.vector.scalar_tensor_tensor(
+                out=z_rows[a][:, cols], in0=h_rows[a][:, cols], scalar=gain[:, a : a + 1], in1=sg_rows[a][:, cols],
+                op0=ALU.mult, op1=ALU.mult,
+            )
+            nc.tensor.transpose(turn_banks[jh][:, a, :], z_rows[a][:, cols], ident_bf[:])
+
+        def turn_out(pair, jh):
+            nc.vector.tensor_copy(
+                out=z_turned[jh][:, :, 64 * pair : 64 * (pair + 1)],
+                in_=turn_banks[jh][:, 2 * pair : 2 * pair + 2, :].rearrange("j a i -> j (a i)").bitcast(F32).rearrange("j (p u) -> j u p", u=2),
+            )
+
+        for jh in range(2):
+            cols = slice(jh * P, (jh + 1) * P)
+            banks = [psum.tile([P, P], F32, name=f"h_bank{a}_{jh}", tag=f"bank{4 * jh + a}") for a in range(2)]
+            for a in range(2):
+                for c in range(3):
+                    first_pass(banks[a][:], code_words, first_planes, c, a, cols)
+            for a in range(2):
+                nc.scalar.activation(out=h_rows[a][:, cols], in_=banks[a][:], func=ACT.Copy, scale=0.0625)
+            for a in range(2):
+                nc.scalar.activation(
+                    out=ds_rows[a][:].indirect(n1_list[:, 8 * jh : 8 * (jh + 1)]), in_=h_rows[a][:, cols], func=ACT.Copy
+                )
+        gather_scales("second_picked", "picked_scales", [(c, d_scale_table, code_half(c, 1)) for c in range(3)], second_planes)
+        code_words = [gather_words(f"code_words{c}_1", f"code_words{c}", d_word_table, code_half(c, 1)) for c in range(3)]
+        for a in range(2, 4):
+            bank = psum.tile([P, S], F32, name=f"h_bank{a}", tag=f"bank{a}")
+            for c in range(3):
+                first_pass(bank[:], code_words, second_planes, c, a - 2, slice(0, S))
+            nc.vector.tensor_scalar(out=h_rows[a][:], in0=bank[:], scalar1=0.0625, scalar2=None, op0=ALU.mult)
+            nc.scalar.activation(out=ds_rows[a][:].indirect(n1_list[:]), in_=h_rows[a][:], func=ACT.Copy)
+        z_pairs = [
+            keep.tile([P, 2, S], BF16, name="z_first", tag="code_words2", align_bytes=64),
+            keep.tile([P, 2, S], BF16, name="z_second"),
+        ]
+        z_rows = [z_pairs[a // 2][:, a % 2, :] for a in range(4)]
+        turn_banks = [psum.tile([P, 4, P], BF16, name=f"turn_bank{jh}", tag=f"bank{2 + jh}") for jh in range(2)]
+        for jh in range(2):
+            for a in range(2):
+                gate(a, jh)
+            turn_out(0, jh)
+        gather_scales("two_picked", "code_words1", [(0, x_scale_table, two_list[:])], two_plane)
+        two_words = gather_words("two_words", "token_words2", x_word_table, two_list[:])
+
+        w_words = [keep.tile([P, 2 * P], U32, name=f"w_words{b}", align_bytes=64) for b in range(4)]
+        w_planes = [keep.tile([P, 2 * P], U8, name=f"w_planes{b}", align_bytes=64) for b in range(4)]
+
+        def quantise_weights(b):
+            grouped = keep.tile([P, 2, P, 4], BF16, name=f"w_grouped{b}", tag="w_grouped" if b == 0 else "z_grouped1", align_bytes=64)
+            for which in range(2):
+                nc.vector.tensor_copy(
+                    out=grouped[:, which].rearrange("p (c i) t -> p c t i", i=4),
+                    in_=w_raw[which][:, :, b * P : (b + 1) * P].rearrange("p t (c i) -> p c t i", i=4),
+                )
+            nc.vector.quantize_mx(
+                out=w_words[b][:].bitcast(FP8X4), scales=w_planes[b][:], in_=grouped[:].rearrange("p w m t -> p (w m t)")
+            )
+
+        quantise_weights(0)
+
+        z_words = [keep.tile([P, P], U32, name=f"z_words{jh}", align_bytes=64) for jh in range(2)]
+        z_planes = [keep.tile([P, P], U8, name=f"z_planes{jh}", align_bytes=64) for jh in range(2)]
+        for jh in range(2):
+            for a in range(2, 4):
+                gate(a, jh)
+            turn_out(1, jh)
+            back_bank = psum.tile([P, 2, P], F32, name=f"back_bank{jh}", tag=f"back_bank{jh}")
+            for u in range(2):
+                nc.tensor.transpose(back_bank[:, u, :], z_turned[jh][:, u, :], ident_f32[:])
+            z_grouped = keep.tile([P, P, 4], BF16, name=f"z_grouped{jh}", tag=f"z_grouped{jh}", align_bytes=64)
+            nc.vector.tensor_copy(
+                out=z_grouped[:].rearrange("p j t -> p (j t)").bitcast(F32).rearrange("p (j u) -> p j u", u=2),
+                in_=back_bank[:].rearrange("p u j -> p j u"),
+            )
+            nc.vector.quantize_mx(
+                out=z_words[jh][:].bitcast(FP8X4), scales=z_planes[jh][:], in_=z_grouped[:].rearrange("p j t -> p (j t)")
+            )
+
+        for b in range(4):
+            if b > 0:
+                quantise_weights(b)
+            bank = psum.tile([P, S], F32, name=f"h2_bank{b}", tag=f"bank{b if b < 2 else b + 2}")
+            for jh in range(2):
+                cols = slice(jh * P, (jh + 1) * P)
+                nc.tensor.matmul_mx(
+                    out=bank[:, cols],
+                    lhsT=w_words[b][:, P:].bitcast(FP8X4),
+                    lhsT_scale=w_planes[b][:, P:],
+                    rhs=two_words[:, cols].bitcast(FP8X4),
+                    rhs_scale=two_plane[:, cols],
+                    start=True,
+                    stop=False,
+                )
+                nc.tensor.matmul_mx(
+                    out=bank[:, cols],
+                    lhsT=w_words[b][:, :P].bitcast(FP8X4),
+                    lhsT_scale=w_planes[b][:, :P],
+                    rhs=z_words[jh][:].bitcast(FP8X4),
+                    rhs_scale=z_planes[jh][:],
+                    start=False,
+                    stop=True,
+                )
+            h2 = keep.tile([P, S], F32, name=f"h2_{b}")
+            if b == 0:
+                nc.scalar.activation(out=h2[:], in_=bank[:], func=ACT.Copy)
+            else:
+                nc.vector.tensor_copy(out=h2[:], in_=bank[:])
+            pa = keep.tile([P, W], F32, name=f"pa{b}")
+            pb = keep.tile([P, W], F32, name=f"pb{b}")
+            rb = keep.tile([P, W], F32, name=f"rb{b}")
+            ub = keep.tile([P, S], F32, name=f"ub{b}")
+            less = keep.tile([P, S], F32, name=f"less{b}")
+            result = keep.tile([P, S], F32, name=f"result{b}")
+            nc.scalar.activation(out=pb[:], in_=h2[:].indirect(n4_list[:]), func=ACT.Copy)
+            nc.scalar.activation(out=pa[:], in_=h2[:].indirect(n3_list[:]), func=ACT.Copy)
+            nc.vector.tensor_tensor(out=rb[:], in0=pa[:], in1=pb[:], op=ALU.max)
+            nc.scalar.activation(out=ub[:].indirect(n5_list[:]), in_=pb[:], func=ACT.Copy)
+            nc.scalar.activation(out=less[:, :P], in_=h2[:].indirect(n7_list[:, :8]), func=ACT.Copy)
+            nc.scalar.activation(out=ub[:].indirect(n6_list[:]), in_=rb[:], func=ACT.Copy)
+            nc.scalar.activation(out=less[:, P:], in_=h2[:].indirect(n7_list[:, 8:]), func=ACT.Copy)
+            for cols in [slice(0, P), slice(P, S)] if b == 3 else [slice(0, S)]:
+                nc.vector.tensor_tensor(out=result[:, cols], in0=ub[:, cols], in1=less[:, cols], op=ALU.subtract)
+                nc.sync.dma_start(out=out[b * P : (b + 1) * P, cols], in_=result[:, cols])

@@ -57,6 +57,8 @@ def tile_picked_mthhznterlcpsw_none_p_kernel(
         nc.gpsimd.memset(vector_rows[:], 0.0)
         ident_f32 = keep.tile([P, P], F32, name="ident_f32")
         make_identity(nc, ident_f32[:])
+        warm = keep.tile([P, 1], F32, name="warm")
+        nc.scalar.activation(out=warm[:], in_=ident_f32[:, 0:1], func=ACT.Sigmoid)
         for v, src in enumerate((sl, th, gn)):
             nc.gpsimd.dma_start(out=vector_rows[4 * v : 4 * v + 4, :], in_=src.rearrange("(a p) o -> a (p o)", p=P))
         ident_bf = keep.tile([P, P], BF16, name="ident_bf")

@@ -27,6 +27,7 @@ def tile_picked_mthhznterlcpsw_none_p_kernel(
     with ExitStack() as ctx:
         lists = ctx.enter_context(tc.tile_pool(name="lists", bufs=1))
         keep = ctx.enter_context(tc.tile_pool(name="keep", bufs=1))
+        shared = ctx.enter_context(tc.tile_pool(name="shared", bufs=1))
         psum = ctx.enter_context(tc.psum_pool(name="psum", bufs=1))
 
         def load_list(name, src):
@@ -42,60 +43,69 @@ def tile_picked_mthhznterlcpsw_none_p_kernel(
 
         def load_word_table(name, src, cols):
             tile = keep.tile([P, cols], I32, name=name)
-            nc.sync.dma_start(out=tile[:], in_=src[0].rearrange("p c r -> p (c r)").bitcast(I32))
+            nc.scalar.dma_start(out=tile[:], in_=src[0].rearrange("p c r -> p (c r)").bitcast(I32))
             return tile
 
         x_scale_table = load_scale_table("x_scale_table", x_scales, T)
         d_scale_table = load_scale_table("d_scale_table", d_scales, G)
+        vector_rows = keep.tile([P, P], F32, name="vector_rows")
+        nc.gpsimd.memset(vector_rows[:], 0.0)
+
+        def load_row_vector(v, src):
+            nc.scalar.dma_start(out=vector_rows[4 * v : 4 * v + 4, :], in_=src.rearrange("(a p) o -> a (p o)", p=P))
+
+        load_row_vector(0, sl)
+        d_word_table = load_word_table("d_word_table", d_words, G)
+        x_word_table = load_word_table("x_word_table", x_words, T)
+        load_row_vector(1, th)
+        load_row_vector(2, gn)
         token_lists = [load_list("offs", offs)]
         code_lists = [load_list("k1", k1), load_list("k2", k2), load_list("k3", k3)]
         token_lists += [load_list("hz", hz), load_list("hy", hy)]
-        d_word_table = load_word_table("d_word_table", d_words, G)
-        x_word_table = load_word_table("x_word_table", x_words, T)
 
-        vector_rows = keep.tile([P, P], F32, name="vector_rows")
-        nc.gpsimd.memset(vector_rows[:], 0.0)
         ident_f32 = keep.tile([P, P], F32, name="ident_f32")
         make_identity(nc, ident_f32[:])
         warm = keep.tile([P, 1], F32, name="warm")
         nc.scalar.activation(out=warm[:], in_=ident_f32[:, 0:1], func=ACT.Sigmoid)
-        for v, src in enumerate((sl, th, gn)):
-            nc.gpsimd.dma_start(out=vector_rows[4 * v : 4 * v + 4, :], in_=src.rearrange("(a p) o -> a (p o)", p=P))
         ident_bf = keep.tile([P, P], BF16, name="ident_bf")
-        make_identity(nc, ident_bf[:])
+        nc.vector.tensor_copy(out=ident_bf[:], in_=ident_f32[:])
         vector_bank = psum.tile([P, P], F32, name="vector_bank", tag="back_bank0")
         nc.tensor.transpose(vector_bank[:], vector_rows[:], ident_f32[:])
         per_row = keep.tile([P, 12], F32, name="per_row")
         nc.scalar.activation(out=per_row[:], in_=vector_bank[:, :12], func=ACT.Copy)
         slope, thresh, gain = per_row[:, 0:4], per_row[:, 4:8], per_row[:, 8:12]
 
-        first_planes = keep.tile([P, 6 * HALF], U8, name="first_planes", align_bytes=64)
+        first_planes = keep.tile([P, 3 * HALF + 3 * P], U8, name="first_planes", align_bytes=64)
+        later_token_planes = keep.tile([P, 3 * P], U8, name="later_token_planes", align_bytes=64)
         second_planes = keep.tile([P, 3 * HALF], U8, name="second_planes", align_bytes=64)
         two_plane = keep.tile([P, S], U8, name="two_plane", align_bytes=64)
-        for planes in (first_planes, second_planes, two_plane):
+        for planes in (first_planes, later_token_planes, second_planes, two_plane):
             nc.vector.memset(planes[:].bitcast(I32), 0)
 
-        def gather_scales(name, tag, picks, planes):
-            picked = keep.tile([P, len(picks) * HALF], U8, name=name, tag=tag, align_bytes=64)
-            for c, table, offsets in picks:
-                nc.vector.tensor_copy(out=picked[:, c * HALF : (c + 1) * HALF], in_=table[:].indirect(offsets))
+        def gather_scales(picked, picks, planes):
+            for start, table, offsets in picks:
+                width = 16 * offsets.shape[1]
+                nc.vector.tensor_copy(out=picked[:, start : start + width], in_=table[:].indirect(offsets))
             for j in range(4):
                 nc.sync.dma_start(out=planes[j:P:32, :].bitcast(I32), in_=picked[8 * j : P : 32, :].bitcast(I32))
 
-        def gather_words(name, tag, table, offsets):
-            picked = keep.tile([P, HALF], U32, name=name, tag=tag, align_bytes=64)
-            nc.vector.tensor_copy(out=picked[:], in_=table[:].bitcast(U32).indirect(offsets))
+        def load_weights(name, w):
+            raw = keep.tile([P, 4, N], F32, name=name)
+            nc.sync.dma_start(out=raw[:], in_=w.rearrange("(p t) m -> p t m", t=4))
+            return raw
+
+        def gather_words(picked, table, offsets):
+            nc.vector.tensor_copy(out=picked, in_=table[:].bitcast(U32).indirect(offsets))
             return picked
 
         def code_half(c, half):
             return code_lists[c][:, 16 * half : 16 * (half + 1)]
 
         gather_scales(
-            "first_picked",
-            "picked_scales",
-            [(3, x_scale_table, token_lists[0][:])]
-            + [(c, d_scale_table, code_half(c, 0)) for c in range(3)]
-            + [(3 + c, x_scale_table, token_lists[c][:]) for c in (1, 2)],
+            shared.tile([P, 3 * HALF + 3 * P], U8, name="first_picked", offset=2816, align_bytes=64),
+            [(3 * HALF, x_scale_table, token_lists[0][:, :8])]
+            + [(c * HALF, d_scale_table, code_half(c, 0)) for c in range(3)]
+            + [(3 * HALF + c * P, x_scale_table, token_lists[c][:, :8]) for c in (1, 2)],
             first_planes,
         )
         n1_list = load_list("n1", n1)
@@ -103,50 +113,45 @@ def tile_picked_mthhznterlcpsw_none_p_kernel(
         two_list = load_list("two", two)
         n4_list = load_list("n4", n4)
         n3_list = load_list("n3", n3)
-        n5_list = load_list("n5", n5)
-        n7_list = load_list("n7", n7)
-        n6_list = load_list("n6", n6)
-        w_raw = []
-        for name, w in (("w1_raw", w1), ("w2_raw", w2)):
-            raw = keep.tile([P, 4, N], F32, name=name)
-            nc.sync.dma_start(out=raw[:], in_=w.rearrange("(p t) m -> p t m", t=4))
-            w_raw.append(raw)
-        code_words = [gather_words(f"code_words{c}_0", f"code_words{c}", d_word_table, code_half(c, 0)) for c in range(3)]
-        token_words = [keep.tile([P, S], U32, name=f"token_words{c}", tag=f"token_words{c}", align_bytes=64) for c in range(3)]
-        for jh in range(2):
-            for c in range(3):
-                nc.vector.tensor_copy(
-                    out=token_words[c][:, jh * P : (jh + 1) * P],
-                    in_=x_word_table[:].bitcast(U32).indirect(token_lists[c][:, 8 * jh : 8 * (jh + 1)]),
-                )
-        token_planes = [first_planes[:, (3 + c) * HALF : (4 + c) * HALF] for c in range(3)]
+        w_raw = [load_weights("w1_raw", w1)]
+        gather_scales(
+            keep.tile([P, 3 * P], U8, name="later_tokens_picked"),
+            [(c * P, x_scale_table, token_lists[c][:, 8:]) for c in range(3)],
+            later_token_planes,
+        )
+        w_raw.append(load_weights("w2_raw", w2))
+        first_codes = keep.tile([P, 3, HALF], U32, name="first_codes", align_bytes=64)
+        first_tokens = keep.tile([P, 3, P], U32, name="first_tokens", align_bytes=64)
+        code_words = [gather_words(first_codes[:, c, :], d_word_table, code_half(c, 0)) for c in range(3)]
+        token_words = [[gather_words(first_tokens[:, c, :], x_word_table, token_lists[c][:, :8]) for c in range(3)]]
+        token_planes = [first_planes[:, 3 * HALF :], later_token_planes[:]]
 
         slope_thresh = keep.tile([P, 4], F32, name="slope_thresh")
         bias = keep.tile([P, 4], F32, name="bias")
         nc.gpsimd.tensor_tensor(out=slope_thresh[:], in0=slope, in1=thresh, op=ALU.mult)
         nc.gpsimd.tensor_scalar(out=bias[:], in0=slope_thresh[:], scalar1=-1.0, scalar2=0.0, op0=ALU.mult, op1=ALU.add)
 
-        h_rows = [keep.tile([P, S], F32, name=f"h_rows{a}") for a in range(4)]
+        h_rows = [keep.tile([P, S], F32, name=f"h_rows{a}", tag=f"h_rows{a}", align_bytes=64) for a in range(4)]
         ds_rows = [keep.tile([P, 2 * S], F32, name=f"ds_rows{a}") for a in range(4)]
         sg_rows = [keep.tile([P, S], F32, name=f"sg_rows{a}") for a in range(4)]
         z_turned = [keep.tile([P, 2, P], F32, name=f"z_turned{jh}") for jh in range(2)]
 
-        def first_pass(bank, words, planes, c, r, cols):
+        def first_pass(bank, words, planes, c, r, jh):
             nc.tensor.matmul_mx(
                 out=bank,
                 lhsT=words[c][:, r * P : (r + 1) * P].bitcast(FP8X4),
                 lhsT_scale=planes[:, c * HALF + r * P : c * HALF + (r + 1) * P],
-                rhs=token_words[c][:, cols].bitcast(FP8X4),
-                rhs_scale=token_planes[c][:, cols],
+                rhs=token_words[jh][c].bitcast(FP8X4),
+                rhs_scale=token_planes[jh][:, c * P : (c + 1) * P],
                 start=(c == 0),
                 stop=(c == 2),
             )
 
-        def gate(a, jh):
-            cols = slice(jh * P, (jh + 1) * P)
+        def gate(a, halves):
+            cols = slice(halves[0] * P, (halves[-1] + 1) * P)
             nc.scalar.activation(
                 out=sg_rows[a][:, cols],
-                in_=ds_rows[a][:].indirect(n2_list[:, 8 * jh : 8 * (jh + 1)]),
+                in_=ds_rows[a][:].indirect(n2_list[:, cols.start // 16 : cols.stop // 16]),
                 func=ACT.Sigmoid,
                 scale=slope[:, a : a + 1],
                 bias=bias[:, a : a + 1],
@@ -155,7 +160,8 @@ def tile_picked_mthhznterlcpsw_none_p_kernel(
                 out=z_rows[a][:, cols], in0=h_rows[a][:, cols], scalar=gain[:, a : a + 1], in1=sg_rows[a][:, cols],
                 op0=ALU.mult, op1=ALU.mult,
             )
-            nc.tensor.transpose(turn_banks[jh][:, a, :], z_rows[a][:, cols], ident_bf[:])
+            for jh in halves:
+                nc.tensor.transpose(turn_banks[jh][:, a, :], z_rows[a][:, jh * P : (jh + 1) * P], ident_bf[:])
 
         def turn_out(pair, jh):
             nc.vector.tensor_copy(
@@ -163,66 +169,79 @@ def tile_picked_mthhznterlcpsw_none_p_kernel(
                 in_=turn_banks[jh][:, 2 * pair : 2 * pair + 2, :].rearrange("j a i -> j (a i)").bitcast(F32).rearrange("j (p u) -> j u p", u=2),
             )
 
-        for jh in range(2):
+        def first_rows(jh):
             cols = slice(jh * P, (jh + 1) * P)
             banks = [psum.tile([P, P], F32, name=f"h_bank{a}_{jh}", tag=f"bank{4 * jh + a}") for a in range(2)]
             for a in range(2):
                 for c in range(3):
-                    first_pass(banks[a][:], code_words, first_planes, c, a, cols)
+                    first_pass(banks[a][:], code_words, first_planes, c, a, jh)
             for a in range(2):
                 nc.scalar.activation(out=h_rows[a][:, cols], in_=banks[a][:], func=ACT.Copy, scale=0.0625)
             for a in range(2):
                 nc.scalar.activation(
                     out=ds_rows[a][:].indirect(n1_list[:, 8 * jh : 8 * (jh + 1)]), in_=h_rows[a][:, cols], func=ACT.Copy
                 )
-        gather_scales("second_picked", "picked_scales", [(c, d_scale_table, code_half(c, 1)) for c in range(3)], second_planes)
-        code_words = [gather_words(f"code_words{c}_1", f"code_words{c}", d_word_table, code_half(c, 1)) for c in range(3)]
+
+        first_rows(0)
+        gather_scales(
+            shared.tile([P, 3 * HALF], U8, name="second_picked", offset=3072, align_bytes=64),
+            [(c * HALF, d_scale_table, code_half(c, 1)) for c in range(3)],
+            second_planes,
+        )
+        n5_list = load_list("n5", n5)
+        n7_list = load_list("n7", n7)
+        n6_list = load_list("n6", n6)
+        second_tokens = shared.tile([P, 3, P], U32, name="second_tokens", offset=3840, align_bytes=64)
+        token_words.append([gather_words(second_tokens[:, c, :], x_word_table, token_lists[c][:, 8:]) for c in range(3)])
+        first_rows(1)
+        second_codes = shared.tile([P, 3, HALF], U32, name="second_codes", offset=0, align_bytes=64)
+        code_words = [gather_words(second_codes[:, c, :], d_word_table, code_half(c, 1)) for c in range(3)]
         for a in range(2, 4):
             bank = psum.tile([P, S], F32, name=f"h_bank{a}", tag=f"bank{a}")
-            for c in range(3):
-                first_pass(bank[:], code_words, second_planes, c, a - 2, slice(0, S))
+            for jh in range(2):
+                for c in range(3):
+                    first_pass(bank[:, jh * P : (jh + 1) * P], code_words, second_planes, c, a - 2, jh)
             nc.vector.tensor_scalar(out=h_rows[a][:], in0=bank[:], scalar1=0.0625, scalar2=None, op0=ALU.mult)
             nc.scalar.activation(out=ds_rows[a][:].indirect(n1_list[:]), in_=h_rows[a][:], func=ACT.Copy)
         z_pairs = [
-            keep.tile([P, 2, S], BF16, name="z_first", tag="code_words2", align_bytes=64),
+            shared.tile([P, 2, S], BF16, name="z_first", offset=0, align_bytes=64),
             keep.tile([P, 2, S], BF16, name="z_second"),
         ]
         z_rows = [z_pairs[a // 2][:, a % 2, :] for a in range(4)]
         turn_banks = [psum.tile([P, 4, P], BF16, name=f"turn_bank{jh}", tag=f"bank{2 + jh}") for jh in range(2)]
+        for a in range(2):
+            gate(a, [0, 1])
         for jh in range(2):
-            for a in range(2):
-                gate(a, jh)
             turn_out(0, jh)
-        gather_scales("two_picked", "code_words1", [(0, x_scale_table, two_list[:])], two_plane)
-        two_words = gather_words("two_words", "token_words2", x_word_table, two_list[:])
+        gather_scales(keep.tile([P, S], U8, name="two_picked", tag="h_rows0", align_bytes=64), [(0, x_scale_table, two_list[:])], two_plane)
+        two_words = gather_words(keep.tile([P, S], U32, name="two_words", tag="h_rows1", align_bytes=64)[:], x_word_table, two_list[:])
 
         w_words = [keep.tile([P, 2 * P], U32, name=f"w_words{b}", align_bytes=64) for b in range(4)]
         w_planes = [keep.tile([P, 2 * P], U8, name=f"w_planes{b}", align_bytes=64) for b in range(4)]
 
-        def quantise_weights(b):
-            grouped = keep.tile([P, 2, P, 4], BF16, name=f"w_grouped{b}", tag="w_grouped" if b == 0 else "z_grouped1", align_bytes=64)
+        def quantise_weights(b, grouped):
             for which in range(2):
                 nc.vector.tensor_copy(
                     out=grouped[:, which].rearrange("p (c i) t -> p c t i", i=4),
                     in_=w_raw[which][:, :, b * P : (b + 1) * P].rearrange("p t (c i) -> p c t i", i=4),
                 )
             nc.vector.quantize_mx(
-                out=w_words[b][:].bitcast(FP8X4), scales=w_planes[b][:], in_=grouped[:].rearrange("p w m t -> p (w m t)")
+                out=w_words[b][:].bitcast(FP8X4), scales=w_planes[b][:], in_=grouped.rearrange("p w m t -> p (w m t)")
             )
 
-        quantise_weights(0)
+        quantise_weights(0, keep.tile([P, 2, P, 4], BF16, name="first_grouped", align_bytes=64)[:])
 
         z_words = [keep.tile([P, P], U32, name=f"z_words{jh}", align_bytes=64) for jh in range(2)]
         z_planes = [keep.tile([P, P], U8, name=f"z_planes{jh}", align_bytes=64) for jh in range(2)]
         for jh in range(2):
             for a in range(2, 4):
-                gate(a, jh)
+                gate(a, [jh])
             turn_out(1, jh)
             back_bank = psum.tile([P, 2, P], F32, name=f"back_bank{jh}", tag=f"back_bank{jh}")
             for u in range(2):
                 nc.tensor.transpose(back_bank[:, u, :], z_turned[jh][:, u, :], ident_f32[:])
             z_grouped = keep.tile([P, P, 4], BF16, name=f"z_grouped{jh}", tag=f"z_grouped{jh}", align_bytes=64)
-            nc.vector.tensor_copy(
+            (nc.vector.tensor_copy if jh == 0 else nc.scalar.copy)(
                 out=z_grouped[:].rearrange("p j t -> p (j t)").bitcast(F32).rearrange("p (j u) -> p j u", u=2),
                 in_=back_bank[:].rearrange("p u j -> p j u"),
             )
@@ -230,14 +249,19 @@ def tile_picked_mthhznterlcpsw_none_p_kernel(
                 out=z_words[jh][:].bitcast(FP8X4), scales=z_planes[jh][:], in_=z_grouped[:].rearrange("p j t -> p (j t)")
             )
 
+        later_grouped = keep.tile([P, 3, 2, P, 4], BF16, name="later_grouped", tag="z_grouped1", align_bytes=64)
         for b in range(4):
-            if b > 0:
-                quantise_weights(b)
-            bank = psum.tile([P, S], F32, name=f"h2_bank{b}", tag=f"bank{b if b < 2 else b + 2}")
+            h2 = keep.tile([P, S], F32, name=f"h2_{b}")
+            if b == 0:
+                sums = [psum.tile([P, P], F32, name=f"h2_bank0_{jh}", tag=f"bank{jh}")[:] for jh in range(2)]
+            else:
+                quantise_weights(b, later_grouped[:, b - 1])
+                bank = psum.tile([P, S], F32, name=f"h2_bank{b}", tag=f"bank{(4, 5, 0)[b - 1]}")
+                sums = [bank[:, :P], bank[:, P:]]
             for jh in range(2):
                 cols = slice(jh * P, (jh + 1) * P)
                 nc.tensor.matmul_mx(
-                    out=bank[:, cols],
+                    out=sums[jh],
                     lhsT=w_words[b][:, P:].bitcast(FP8X4),
                     lhsT_scale=w_planes[b][:, P:],
                     rhs=two_words[:, cols].bitcast(FP8X4),
@@ -246,7 +270,7 @@ def tile_picked_mthhznterlcpsw_none_p_kernel(
                     stop=False,
                 )
                 nc.tensor.matmul_mx(
-                    out=bank[:, cols],
+                    out=sums[jh],
                     lhsT=w_words[b][:, :P].bitcast(FP8X4),
                     lhsT_scale=w_planes[b][:, :P],
                     rhs=z_words[jh][:].bitcast(FP8X4),
@@ -254,10 +278,9 @@ def tile_picked_mthhznterlcpsw_none_p_kernel(
                     start=False,
                     stop=True,
                 )
-            h2 = keep.tile([P, S], F32, name=f"h2_{b}")
-            if b == 0:
-                nc.scalar.activation(out=h2[:], in_=bank[:], func=ACT.Copy)
-            else:
+                if b == 0:
+                    nc.scalar.activation(out=h2[:, cols], in_=sums[jh], func=ACT.Copy)
+            if b > 0:
                 nc.vector.tensor_copy(out=h2[:], in_=bank[:])
             pa = keep.tile([P, W], F32, name=f"pa{b}")
             pb = keep.tile([P, W], F32, name=f"pb{b}")

from contextlib import ExitStack

import concourse.mybir as mybir
from concourse.masks import make_identity

F32 = mybir.dt.float32
BF16 = mybir.dt.bfloat16
I32 = mybir.dt.int32
U32 = mybir.dt.uint32
U16 = mybir.dt.uint16
U8 = mybir.dt.uint8
FP8X4 = mybir.dt.float8_e4m3fn_x4
ALU = mybir.AluOpType
ACT = mybir.ActivationFunctionType

P = 128
K, T, S, N, G, H, W = 512, 1024, 256, 512, 2048, 512, 128
HALF = 256
FLOPS = 2 * (3 * K * H * S + H * N * S + K * N * S)


def tile_picked_mthhznterlcpsw_none_p_kernel(
    tc, x_words, x_scales, d_words, d_scales, sl, th, gn, w1, w2,
    offs, k1, hz, k2, hy, k3, n1, n2, two, n3, n4, n5, n6, n7, out,
):
    nc = tc.nc
    with ExitStack() as ctx:
        lists = ctx.enter_context(tc.tile_pool(name="lists", bufs=1))
        keep = ctx.enter_context(tc.tile_pool(name="keep", bufs=1))
        shared = ctx.enter_context(tc.tile_pool(name="shared", bufs=1))
        psum = ctx.enter_context(tc.psum_pool(name="psum", bufs=1))

        def load_list(name, src):
            tile = lists.tile(list(src.shape), U16, name=name)
            nc.sync.dma_start(out=tile[:], in_=src)
            return tile

        def load_scale_table(name, src, cols):
            tile = keep.tile([P, cols], U8, name=name)
            rows = src[0].bitcast(I32).unsqueeze(1).broadcast_to([16, 8, cols // 4])
            nc.scalar.dma_start(out=tile[:].bitcast(I32), in_=rows)
            return tile

        def load_word_table(name, src, cols):
            tile = keep.tile([P, cols], I32, name=name)
            nc.scalar.dma_start(out=tile[:], in_=src[0].rearrange("p c r -> p (c r)").bitcast(I32))
            return tile

        x_scale_table = load_scale_table("x_scale_table", x_scales, T)
        d_scale_table = load_scale_table("d_scale_table", d_scales, G)
        vector_rows = keep.tile([P, P], F32, name="vector_rows")
        nc.gpsimd.memset(vector_rows[:], 0.0)

        def load_row_vector(v, src):
            nc.scalar.dma_start(out=vector_rows[4 * v : 4 * v + 4, :], in_=src.rearrange("(a p) o -> a (p o)", p=P))

        load_row_vector(0, sl)
        d_word_table = load_word_table("d_word_table", d_words, G)
        x_word_table = load_word_table("x_word_table", x_words, T)
        load_row_vector(1, th)
        load_row_vector(2, gn)
        token_lists = [load_list("offs", offs)]
        code_lists = [load_list("k1", k1), load_list("k2", k2), load_list("k3", k3)]
        token_lists += [load_list("hz", hz), load_list("hy", hy)]

        ident_f32 = keep.tile([P, P], F32, name="ident_f32")
        make_identity(nc, ident_f32[:])
        warm = keep.tile([P, 1], F32, name="warm")
        nc.scalar.activation(out=warm[:], in_=ident_f32[:, 0:1], func=ACT.Sigmoid)
        ident_bf = keep.tile([P, P], BF16, name="ident_bf")
        nc.vector.tensor_copy(out=ident_bf[:], in_=ident_f32[:])
        vector_bank = psum.tile([P, P], F32, name="vector_bank", tag="back_bank0")
        nc.tensor.transpose(vector_bank[:], vector_rows[:], ident_f32[:])
        per_row = keep.tile([P, 12], F32, name="per_row")
        nc.scalar.activation(out=per_row[:], in_=vector_bank[:, :12], func=ACT.Copy)
        slope, thresh, gain = per_row[:, 0:4], per_row[:, 4:8], per_row[:, 8:12]

        first_planes = keep.tile([P, 3 * HALF + 3 * P], U8, name="first_planes", align_bytes=64)
        later_token_planes = keep.tile([P, 3 * P], U8, name="later_token_planes", align_bytes=64)
        second_planes = keep.tile([P, 3 * HALF], U8, name="second_planes", align_bytes=64)
        two_plane = keep.tile([P, S], U8, name="two_plane", align_bytes=64)
        for planes in (first_planes, later_token_planes, second_planes, two_plane):
            nc.vector.memset(planes[:].bitcast(I32), 0)

        def gather_scales(picked, picks, planes):
            for start, table, offsets in picks:
                width = 16 * offsets.shape[1]
                nc.vector.tensor_copy(out=picked[:, start : start + width], in_=table[:].indirect(offsets))
            for j in range(4):
                nc.sync.dma_start(out=planes[j:P:32, :].bitcast(I32), in_=picked[8 * j : P : 32, :].bitcast(I32))

        def load_weights(name, w):
            raw = keep.tile([P, 4, N], F32, name=name)
            nc.sync.dma_start(out=raw[:], in_=w.rearrange("(p t) m -> p t m", t=4))
            return raw

        def gather_words(picked, table, offsets):
            nc.vector.tensor_copy(out=picked, in_=table[:].bitcast(U32).indirect(offsets))
            return picked

        def code_half(c, half):
            return code_lists[c][:, 16 * half : 16 * (half + 1)]

        gather_scales(
            shared.tile([P, 3 * HALF + 3 * P], U8, name="first_picked", offset=2816, align_bytes=64),
            [(3 * HALF, x_scale_table, token_lists[0][:, :8])]
            + [(c * HALF, d_scale_table, code_half(c, 0)) for c in range(3)]
            + [(3 * HALF + c * P, x_scale_table, token_lists[c][:, :8]) for c in (1, 2)],
            first_planes,
        )
        n1_list = load_list("n1", n1)
        n2_list = load_list("n2", n2)
        two_list = load_list("two", two)
        n4_list = load_list("n4", n4)
        n3_list = load_list("n3", n3)
        w_raw = [load_weights("w1_raw", w1)]
        gather_scales(
            keep.tile([P, 3 * P], U8, name="later_tokens_picked"),
            [(c * P, x_scale_table, token_lists[c][:, 8:]) for c in range(3)],
            later_token_planes,
        )
        w_raw.append(load_weights("w2_raw", w2))
        first_codes = keep.tile([P, 3, HALF], U32, name="first_codes", align_bytes=64)
        first_tokens = keep.tile([P, 3, P], U32, name="first_tokens", align_bytes=64)
        code_words = [gather_words(first_codes[:, c, :], d_word_table, code_half(c, 0)) for c in range(3)]
        token_words = [[gather_words(first_tokens[:, c, :], x_word_table, token_lists[c][:, :8]) for c in range(3)]]
        token_planes = [first_planes[:, 3 * HALF :], later_token_planes[:]]

        slope_thresh = keep.tile([P, 4], F32, name="slope_thresh")
        bias = keep.tile([P, 4], F32, name="bias")
        nc.gpsimd.tensor_tensor(out=slope_thresh[:], in0=slope, in1=thresh, op=ALU.mult)
        nc.gpsimd.tensor_scalar(out=bias[:], in0=slope_thresh[:], scalar1=-1.0, scalar2=0.0, op0=ALU.mult, op1=ALU.add)

        h_rows = [keep.tile([P, S], F32, name=f"h_rows{a}", tag=f"h_rows{a}", align_bytes=64) for a in range(4)]
        ds_rows = [keep.tile([P, 2 * S], F32, name=f"ds_rows{a}") for a in range(4)]
        sg_rows = [keep.tile([P, S], F32, name=f"sg_rows{a}") for a in range(4)]
        z_turned = [keep.tile([P, 2, P], F32, name=f"z_turned{jh}") for jh in range(2)]

        def first_pass(bank, words, planes, c, r, jh):
            nc.tensor.matmul_mx(
                out=bank,
                lhsT=words[c][:, r * P : (r + 1) * P].bitcast(FP8X4),
                lhsT_scale=planes[:, c * HALF + r * P : c * HALF + (r + 1) * P],
                rhs=token_words[jh][c].bitcast(FP8X4),
                rhs_scale=token_planes[jh][:, c * P : (c + 1) * P],
                start=(c == 0),
                stop=(c == 2),
            )

        def gate(a, halves):
            cols = slice(halves[0] * P, (halves[-1] + 1) * P)
            nc.scalar.activation(
                out=sg_rows[a][:, cols],
                in_=ds_rows[a][:].indirect(n2_list[:, cols.start // 16 : cols.stop // 16]),
                func=ACT.Sigmoid,
                scale=slope[:, a : a + 1],
                bias=bias[:, a : a + 1],
            )
            nc.vector.scalar_tensor_tensor(
                out=z_rows[a][:, cols], in0=h_rows[a][:, cols], scalar=gain[:, a : a + 1], in1=sg_rows[a][:, cols],
                op0=ALU.mult, op1=ALU.mult,
            )
            for jh in halves:
                nc.tensor.transpose(turn_banks[jh][:, a, :], z_rows[a][:, jh * P : (jh + 1) * P], ident_bf[:])

        def turn_out(pair, jh):
            nc.vector.tensor_copy(
                out=z_turned[jh][:, :, 64 * pair : 64 * (pair + 1)],
                in_=turn_banks[jh][:, 2 * pair : 2 * pair + 2, :].rearrange("j a i -> j (a i)").bitcast(F32).rearrange("j (p u) -> j u p", u=2),
            )

        def first_rows(jh):
            cols = slice(jh * P, (jh + 1) * P)
            banks = [psum.tile([P, P], F32, name=f"h_bank{a}_{jh}", tag=f"bank{4 * jh + a}") for a in range(2)]
            for a in range(2):
                for c in range(3):
                    first_pass(banks[a][:], code_words, first_planes, c, a, jh)
            for a in range(2):
                nc.scalar.activation(out=h_rows[a][:, cols], in_=banks[a][:], func=ACT.Copy, scale=0.0625)
            for a in range(2):
                nc.scalar.activation(
                    out=ds_rows[a][:].indirect(n1_list[:, 8 * jh : 8 * (jh + 1)]), in_=h_rows[a][:, cols], func=ACT.Copy
                )

        first_rows(0)
        gather_scales(
            shared.tile([P, 3 * HALF], U8, name="second_picked", offset=3072, align_bytes=64),
            [(c * HALF, d_scale_table, code_half(c, 1)) for c in range(3)],
            second_planes,
        )
        n5_list = load_list("n5", n5)
        n7_list = load_list("n7", n7)
        n6_list = load_list("n6", n6)
        second_tokens = shared.tile([P, 3, P], U32, name="second_tokens", offset=3840, align_bytes=64)
        token_words.append([gather_words(second_tokens[:, c, :], x_word_table, token_lists[c][:, 8:]) for c in range(3)])
        first_rows(1)
        second_codes = shared.tile([P, 3, HALF], U32, name="second_codes", offset=0, align_bytes=64)
        code_words = [gather_words(second_codes[:, c, :], d_word_table, code_half(c, 1)) for c in range(3)]
        for a in range(2, 4):
            bank = psum.tile([P, S], F32, name=f"h_bank{a}", tag=f"bank{a}")
            for jh in range(2):
                for c in range(3):
                    first_pass(bank[:, jh * P : (jh + 1) * P], code_words, second_planes, c, a - 2, jh)
            nc.vector.tensor_scalar(out=h_rows[a][:], in0=bank[:], scalar1=0.0625, scalar2=None, op0=ALU.mult)
            nc.scalar.activation(out=ds_rows[a][:].indirect(n1_list[:]), in_=h_rows[a][:], func=ACT.Copy)
        z_pairs = [
            shared.tile([P, 2, S], BF16, name="z_first", offset=0, align_bytes=64),
            keep.tile([P, 2, S], BF16, name="z_second"),
        ]
        z_rows = [z_pairs[a // 2][:, a % 2, :] for a in range(4)]
        turn_banks = [psum.tile([P, 4, P], BF16, name=f"turn_bank{jh}", tag=f"bank{2 + jh}") for jh in range(2)]
        for a in range(2):
            gate(a, [0, 1])
        for jh in range(2):
            turn_out(0, jh)
        gather_scales(keep.tile([P, S], U8, name="two_picked", tag="h_rows0", align_bytes=64), [(0, x_scale_table, two_list[:])], two_plane)
        two_words = gather_words(keep.tile([P, S], U32, name="two_words", tag="h_rows1", align_bytes=64)[:], x_word_table, two_list[:])

        w_words = [keep.tile([P, 2 * P], U32, name=f"w_words{b}", align_bytes=64) for b in range(4)]
        w_planes = [keep.tile([P, 2 * P], U8, name=f"w_planes{b}", align_bytes=64) for b in range(4)]

        def quantise_weights(b, grouped):
            for which in range(2):
                nc.vector.tensor_copy(
                    out=grouped[:, which].rearrange("p (c i) t -> p c t i", i=4),
                    in_=w_raw[which][:, :, b * P : (b + 1) * P].rearrange("p t (c i) -> p c t i", i=4),
                )
            nc.vector.quantize_mx(
                out=w_words[b][:].bitcast(FP8X4), scales=w_planes[b][:], in_=grouped.rearrange("p w m t -> p (w m t)")
            )

        quantise_weights(0, keep.tile([P, 2, P, 4], BF16, name="first_grouped", align_bytes=64)[:])

        z_words = [keep.tile([P, P], U32, name=f"z_words{jh}", align_bytes=64) for jh in range(2)]
        z_planes = [keep.tile([P, P], U8, name=f"z_planes{jh}", align_bytes=64) for jh in range(2)]
        for jh in range(2):
            for a in range(2, 4):
                gate(a, [jh])
            turn_out(1, jh)
            back_bank = psum.tile([P, 2, P], F32, name=f"back_bank{jh}", tag=f"back_bank{jh}")
            for u in range(2):
                nc.tensor.transpose(back_bank[:, u, :], z_turned[jh][:, u, :], ident_f32[:])
            z_grouped = keep.tile([P, P, 4], BF16, name=f"z_grouped{jh}", tag=f"z_grouped{jh}", align_bytes=64)
            (nc.vector.tensor_copy if jh == 0 else nc.scalar.copy)(
                out=z_grouped[:].rearrange("p j t -> p (j t)").bitcast(F32).rearrange("p (j u) -> p j u", u=2),
                in_=back_bank[:].rearrange("p u j -> p j u"),
            )
            nc.vector.quantize_mx(
                out=z_words[jh][:].bitcast(FP8X4), scales=z_planes[jh][:], in_=z_grouped[:].rearrange("p j t -> p (j t)")
            )

        later_grouped = keep.tile([P, 3, 2, P, 4], BF16, name="later_grouped", tag="z_grouped1", align_bytes=64)
        for b in range(4):
            h2 = keep.tile([P, S], F32, name=f"h2_{b}")
            if b == 0:
                sums = [psum.tile([P, P], F32, name=f"h2_bank0_{jh}", tag=f"bank{jh}")[:] for jh in range(2)]
            else:
                quantise_weights(b, later_grouped[:, b - 1])
                bank = psum.tile([P, S], F32, name=f"h2_bank{b}", tag=f"bank{(4, 5, 0)[b - 1]}")
                sums = [bank[:, :P], bank[:, P:]]
            for jh in range(2):
                cols = slice(jh * P, (jh + 1) * P)
                nc.tensor.matmul_mx(
                    out=sums[jh],
                    lhsT=w_words[b][:, P:].bitcast(FP8X4),
                    lhsT_scale=w_planes[b][:, P:],
                    rhs=two_words[:, cols].bitcast(FP8X4),
                    rhs_scale=two_plane[:, cols],
                    start=True,
                    stop=False,
                )
                nc.tensor.matmul_mx(
                    out=sums[jh],
                    lhsT=w_words[b][:, :P].bitcast(FP8X4),
                    lhsT_scale=w_planes[b][:, :P],
                    rhs=z_words[jh][:].bitcast(FP8X4),
                    rhs_scale=z_planes[jh][:],
                    start=False,
                    stop=True,
                )
                if b == 0:
                    nc.scalar.activation(out=h2[:, cols], in_=sums[jh], func=ACT.Copy)
            if b > 0:
                nc.vector.tensor_copy(out=h2[:], in_=bank[:])
            pa = keep.tile([P, W], F32, name=f"pa{b}")
            pb = keep.tile([P, W], F32, name=f"pb{b}")
            rb = keep.tile([P, W], F32, name=f"rb{b}")
            ub = keep.tile([P, S], F32, name=f"ub{b}")
            less = keep.tile([P, S], F32, name=f"less{b}")
            result = keep.tile([P, S], F32, name=f"result{b}")
            nc.scalar.activation(out=pb[:], in_=h2[:].indirect(n4_list[:]), func=ACT.Copy)
            nc.scalar.activation(out=pa[:], in_=h2[:].indirect(n3_list[:]), func=ACT.Copy)
            nc.vector.tensor_tensor(out=rb[:], in0=pa[:], in1=pb[:], op=ALU.max)
            nc.scalar.activation(out=ub[:].indirect(n5_list[:]), in_=pb[:], func=ACT.Copy)
            nc.scalar.activation(out=less[:, :P], in_=h2[:].indirect(n7_list[:, :8]), func=ACT.Copy)
            nc.scalar.activation(out=ub[:].indirect(n6_list[:]), in_=rb[:], func=ACT.Copy)
            nc.scalar.activation(out=less[:, P:], in_=h2[:].indirect(n7_list[:, 8:]), func=ACT.Copy)
            for cols in [slice(0, P), slice(P, S)] if b == 3 else [slice(0, S)]:
                nc.vector.tensor_tensor(out=result[:, cols], in0=ub[:, cols], in1=less[:, cols], op=ALU.subtract)
                nc.sync.dma_start(out=out[b * P : (b + 1) * P, cols], in_=result[:, cols])
